import numpy as np
import ml_dtypes


def mxq(x, axis, fmt="e4m3"):
    dtype, down = {"e4m3": (ml_dtypes.float8_e4m3fn, 7), "e5m2": (ml_dtypes.float8_e5m2, 14)}[fmt]
    v = np.moveaxis(np.asarray(x, np.float32).astype(ml_dtypes.bfloat16).astype(np.float64), axis, -1)
    blocks = v.reshape(v.shape[:-1] + (-1, 32))
    amax = np.abs(blocks).max(-1, keepdims=True)
    byte = np.maximum(np.where(amax > 0, np.frexp(amax)[1] - 1 + 127, 0) - down, 1)
    scale = np.exp2(byte - 127.0)
    codes = (blocks / scale).astype(np.float32).astype(dtype).astype(np.float64)
    return np.moveaxis((codes * scale).reshape(v.shape), -1, axis)


WIDE = False


def mx_kscale(k):
    if not WIDE:
        return np.ones(k)
    levels = np.array([10, -10, 5, -5, 0])
    if k % 512:
        return np.exp2(np.random.permutation(np.resize(levels, k // 32))).repeat(32)
    a = np.empty((k // 512, 16))
    for p in range(k // 512):
        a[p, :8] = np.random.permutation(np.resize(levels, 8))
        for g in range(8):
            far = levels[np.abs(levels - a[p, g]) >= 10]
            a[p, g + 8] = far[np.random.randint(len(far))]
    return np.exp2(a.ravel()).repeat(32)


def f64(x):
    return np.asarray(x).astype(np.float64)


def striped(idx):
    return np.tile(idx.reshape(-1, 16).T, (8, 1)).astype(np.uint16)


def unstriped(offs):
    return offs[:16].T.reshape(-1).astype(np.int64)


def pack_weight(w):
    k, n = w.shape
    w = f64(np.asarray(w, np.float32).astype(ml_dtypes.bfloat16)).reshape(k // 32, 32, n)
    amax = np.abs(w).max(1)
    byte = np.clip(np.where(amax > 0, np.frexp(amax)[1] - 1 + 127 - 7, 1), 1, 254)
    scaled = (w * np.exp2(127.0 - byte)[:, None, :]).reshape(k, n).astype(np.float32)
    words = np.ascontiguousarray(scaled.reshape(k // 512, 128, 4, n).transpose(0, 1, 3, 2)).astype(ml_dtypes.float8_e4m3fn).view(np.uint8)
    return words, np.ascontiguousarray(byte.astype(np.uint8).reshape(k // 512, 16, n))


def unpack_weight(words, scales):
    g, p, n, _ = words.shape
    vals = np.ascontiguousarray(words).view(ml_dtypes.float8_e4m3fn).astype(np.float64) * np.repeat(np.exp2(scales.astype(np.float64) - 127.0), 8, axis=1)[..., None]
    return vals.transpose(0, 1, 3, 2).reshape(g * 512, n)


def planes(y):
    n, m = y.shape
    v = y.astype(np.float32).astype(ml_dtypes.bfloat16).astype(np.float64).reshape(n // 32, 32, m)
    top = np.abs(v).max(1)
    byte = np.clip(np.where(top > 0, np.frexp(top)[1] - 1 + 127 - 7, 1), 1, 254)
    codes = (v * np.exp2(127.0 - byte)[:, None, :]).reshape(n, m).astype(np.float32).astype(ml_dtypes.float8_e4m3fn).view(np.uint8)
    words = codes.reshape(n // 512, 128, 4, m).transpose(0, 1, 3, 2)
    return np.ascontiguousarray(words), np.ascontiguousarray(byte.astype(np.uint8).reshape(n // 512, 16, m))


def sigmoid(v):
    return 1.0 / (1.0 + np.exp(-np.maximum(v, -700.0)))


K, T, S, W, N = 1024, 1024, 512, 1024, 512


def setup_inputs():
    n = np.random.standard_normal
    s = mx_kscale(K)[:, None]
    packed_xT = pack_weight(n((K, T)) * s)
    packed_eT = pack_weight(n((K, W)) * s)
    return {
        "x_words": packed_xT[0],
        "x_scales": packed_xT[1],
        "e_words": packed_eT[0],
        "e_scales": packed_eT[1],
        "w1": (n((K, N)) / np.sqrt(2 * K) / s).astype(np.float32),
        "w2": (n((K, N)) / np.sqrt(2 * K) / s).astype(np.float32),
        "w3": (n((K, N)) / np.sqrt(2 * K) / s).astype(np.float32),
        "w4": (n((K, N)) / np.sqrt(2 * K) / s).astype(np.float32),
        "offs": striped(np.random.permutation(T)[:S]),
        "tok": striped(np.random.permutation(W)[:S]),
    }


def reference(x_words, x_scales, e_words, e_scales, w1, w2, w3, w4, offs, tok):
    xq = unpack_weight(x_words, x_scales)[:, unstriped(offs)]
    e_tok = unpack_weight(e_words, e_scales)[:, unstriped(tok)]
    g = sigmoid(mxq(f64(w1), 0, "e4m3").T @ xq + mxq(f64(w2), 0, "e4m3").T @ e_tok)
    y = mxq(f64(w3), 0, "e4m3").T @ xq + mxq(f64(w4), 0, "e4m3").T @ e_tok
    out_0 = g * y
    return (out_0,) + planes(out_0)

@@ -1,0 +1,202 @@
+from contextlib import ExitStack
+
+import concourse.mybir as mybir
+
+F32 = mybir.dt.float32
+BF16 = mybir.dt.bfloat16
+I32 = mybir.dt.int32
+U32 = mybir.dt.uint32
+U16 = mybir.dt.uint16
+U8 = mybir.dt.uint8
+FP8X4 = mybir.dt.float8_e4m3fn_x4
+SIGMOID = mybir.ActivationFunctionType.Sigmoid
+MULT = mybir.AluOpType.mult
+
+P = 128
+PACK = 4
+K_PASS = P * PACK
+PASSES = 2
+TABLE = 1024
+S = 512
+M = 512
+QUADS = 4
+JQ = 128
+NQ = S // JQ
+HALF = P // 2
+SCALAR_SHARE = 64
+SCALAR_SHARE_LAST = 20
+
+FLOPS = 4 * 2 * 1024 * M * S
+
+
+def tile_picked_zmtp_sigmoid_po_kernel(
+    tc, x_words, x_scales, e_words, e_scales, w1, w2, w3, w4, offs, tok, out_0, out_1, out_2
+):
+    nc = tc.nc
+    with ExitStack() as ctx:
+        keep = ctx.enter_context(tc.tile_pool(name="keep", bufs=1))
+        psum = ctx.enter_context(tc.psum_pool(name="psum", bufs=1))
+
+        def load_list(src, name):
+            lst = keep.tile([P, S // 16], U16, name=name)
+            nc.sync.dma_start(lst[:], src)
+            return lst
+
+        def load_scale_table(src, name):
+            table = keep.tile([P, TABLE], U8, name=name, align_bytes=64)
+            nc.vector.memset(table[:].bitcast(I32), 0)
+            for quad in range(QUADS):
+                nc.sync.dma_start(
+                    out=table[32 * quad : 32 * quad + 4 * PASSES, :].bitcast(I32),
+                    in_=src[:, 4 * quad : 4 * quad + 4, :].bitcast(I32),
+                )
+            return table
+
+        def load_word_table(src, name):
+            table = keep.tile([P, PASSES, TABLE], U32, name=name, align_bytes=64)
+            nc.sync.dma_start(
+                out=table[:].bitcast(I32),
+                in_=src.rearrange("g p c r -> p g (c r)").bitcast(I32),
+            )
+            return table
+
+        def gather_words(table, lst, name):
+            picked = []
+            for g in range(PASSES):
+                words = keep.tile([P, S], U32, name="%s%d" % (name, g), align_bytes=64)
+                nc.vector.tensor_copy(words[:], table[:, g, :].indirect(lst[:]))
+                picked.append(words)
+            return picked
+
+        def gather_scales(table, lst, name):
+            picked = keep.tile([P, S], U8, name=name, align_bytes=64)
+            nc.vector.tensor_copy(picked[:], table[:].indirect(lst[:]))
+            return picked
+
+        def load_weight(w, g, c0, c1, name):
+            raw = keep.tile([P, PACK, c1 - c0], F32, name=name)
+            rows = w[g * K_PASS : (g + 1) * K_PASS, :].rearrange("(p j) c -> p j c", j=PACK)
+            nc.sync.dma_start(out=raw[:], in_=rows[:, :, c0:c1])
+            return raw
+
+        def weight_tiles(name):
+            grouped = keep.tile([P, PACK, P, PACK], BF16, name=name + "_bf", align_bytes=64)
+            codes = keep.tile([P, M], U32, name=name + "_codes", align_bytes=64)
+            scales = keep.tile([P, M], U8, name=name + "_scales", align_bytes=64)
+            return grouped, codes, scales
+
+        def round_weight(raw, grouped, l0, count, scalar_share):
+            src = raw[:].rearrange("p j (l t) -> p l t j", t=PACK)
+            dst = grouped[:].rearrange("p t l j -> p l t j")
+            nc.scalar.copy(out=dst[:, l0 : l0 + scalar_share], in_=src[:, 0:scalar_share])
+            nc.vector.tensor_copy(out=dst[:, l0 + scalar_share : l0 + count], in_=src[:, scalar_share:count])
+
+        def quantize_whole(tiles):
+            grouped, codes, scales = tiles
+            nc.vector.quantize_mx(
+                out=codes[:].bitcast(FP8X4), scales=scales[:], in_=grouped[:].rearrange("p t l j -> p (t l j)")
+            )
+
+        def quantize_half(tiles, l0):
+            grouped, codes, scales = tiles
+            for t in range(PACK):
+                cols = slice(t * P + l0, t * P + l0 + HALF)
+                nc.vector.quantize_mx(
+                    out=codes[:, cols].bitcast(FP8X4),
+                    scales=scales[:, cols],
+                    in_=grouped[:, t, l0 : l0 + HALF, :].rearrange("p l j -> p (l j)"),
+                )
+
+        def whole_weight(w, g, name):
+            raw = load_weight(w, g, 0, M, name + "_raw")
+            tiles = weight_tiles(name)
+            round_weight(raw, tiles[0], 0, P, SCALAR_SHARE)
+            quantize_whole(tiles)
+            return tiles
+
+        def product(out, tiles, t, words, scales, g, cols, start, stop):
+            nc.tensor.matmul_mx(
+                out=out,
+                lhsT=tiles[1][:, t * P : (t + 1) * P].bitcast(FP8X4),
+                lhsT_scale=tiles[2][:, t * P : (t + 1) * P],
+                rhs=words[g][:, cols].bitcast(FP8X4),
+                rhs_scale=scales[4 * g : P, cols],
+                start=start,
+                stop=stop,
+            )
+
+        gate_banks = [psum.tile([P, S], F32, name="gate_bank%d" % t) for t in range(PACK)]
+        value_banks = [psum.tile([P, PACK, JQ], F32, name="value_bank%d" % q) for q in range(NQ)]
+
+        def gate_pass(tiles, words, scales, g, first, last):
+            for t in range(PACK):
+                product(gate_banks[t][:], tiles, t, words, scales, g, slice(0, S), first, last)
+
+        def value_pass(tiles, words, scales, g, first, last):
+            for q in range(NQ):
+                for t in range(PACK):
+                    product(
+                        value_banks[q][:, t, :], tiles, t, words, scales, g, slice(q * JQ, (q + 1) * JQ),
+                        first and t == 0, last and t == PACK - 1,
+                    )
+
+        w1_0 = whole_weight(w1, 0, "w1_0")
+        x_list = load_list(offs, "x_list")
+        e_list = load_list(tok, "e_list")
+        x_table = load_word_table(x_words, "x_table")
+        x_scale_table = load_scale_table(x_scales, "x_scale_table")
+        x_picked = gather_words(x_table, x_list, "x_picked")
+        x_picked_scales = gather_scales(x_scale_table, x_list, "x_picked_scales")
+        gate_pass(w1_0, x_picked, x_picked_scales, 0, True, False)
+        w1_1 = whole_weight(w1, 1, "w1_1")
+        gate_pass(w1_1, x_picked, x_picked_scales, 1, False, False)
+        e_table = load_word_table(e_words, "e_table")
+        e_scale_table = load_scale_table(e_scales, "e_scale_table")
+        e_picked = gather_words(e_table, e_list, "e_picked")
+        e_picked_scales = gather_scales(e_scale_table, e_list, "e_picked_scales")
+        for g in range(PASSES):
+            w2_g = whole_weight(w2, g, "w2_%d" % g)
+            gate_pass(w2_g, e_picked, e_picked_scales, g, False, g == PASSES - 1)
+
+        gate = keep.tile([P, PACK, S], F32, name="gate")
+        for t in range(PACK):
+            nc.scalar.activation(out=gate[:, t, :], in_=gate_banks[t][:], func=SIGMOID)
+
+        for g in range(PASSES):
+            w3_g = whole_weight(w3, g, "w3_%d" % g)
+            value_pass(w3_g, x_picked, x_picked_scales, g, g == 0, False)
+        w4_0 = whole_weight(w4, 0, "w4_0")
+        value_pass(w4_0, e_picked, e_picked_scales, 0, False, False)
+        w4_1 = weight_tiles("w4_1")
+        for h in range(2):
+            raw = load_weight(w4, 1, h * M // 2, (h + 1) * M // 2, "w4_1_raw%d" % h)
+            round_weight(raw, w4_1[0], h * HALF, HALF, SCALAR_SHARE_LAST)
+            quantize_half(w4_1, h * HALF)
+        value_pass(w4_1, e_picked, e_picked_scales, 1, False, True)
+
+        out_rows = out_0.rearrange("(p t) j -> p t j", t=PACK)
+        out_words = out_1[0].rearrange("p c r -> p (c r)").bitcast(I32)
+        y_codes = keep.tile([P, S], U32, name="y_codes", align_bytes=64)
+        y_scales = keep.tile([P, S], U8, name="y_scales", align_bytes=64)
+        for q in range(NQ):
+            cols = slice(q * JQ, (q + 1) * JQ)
+            y = keep.tile([P, PACK, JQ], F32, name="y%d" % q)
+            nc.vector.tensor_tensor(out=y[:], in0=value_banks[q][:], in1=gate[:, :, cols], op=MULT)
+            nc.sync.dma_start(out=out_rows[:, :, cols], in_=y[:])
+            y_bf = keep.tile([P, JQ, PACK], BF16, name="y_bf%d" % q, align_bytes=64)
+            nc.scalar.copy(
+                out=y_bf[:].rearrange("p (c i) t -> p c t i", i=4),
+                in_=y[:].rearrange("p t (c i) -> p c t i", i=4),
+            )
+            nc.vector.quantize_mx(
+                out=y_codes[:, cols].bitcast(FP8X4), scales=y_scales[:, cols],
+                in_=y_bf[:].rearrange("p c t -> p (c t)"),
+            )
+        for c0, c1 in ((0, S - JQ), (S - JQ, S)):
+            nc.sync.dma_start(out=out_words[:, c0:c1], in_=y_codes[:, c0:c1].bitcast(I32))
+        for quad in range(QUADS):
+            queue = nc.sync if quad % 2 == 0 else nc.scalar
+            queue.dma_start(
+                out=out_2[0, 4 * quad : 4 * quad + 4, :].bitcast(I32),
+                in_=y_scales[32 * quad : 32 * quad + 4, :].bitcast(I32),
+            )

@@ -19,14 +19,22 @@ PASSES = 2
 TABLE = 1024
 S = 512
 M = 512
-QUADS = 4
-JQ = 128
-NQ = S // JQ
-HALF = P // 2
-SCALAR_SHARE = 64
-SCALAR_SHARE_LAST = 20
+QUADRANTS = 4
+PLANE_ROWS = 4
+X_FIRST_ROW = 0
+E_FIRST_ROW = 8
+PART = 128
+PARTS = S // PART
+RUN = 4
 
-FLOPS = 4 * 2 * 1024 * M * S
+EIGHTHS = 8
+W1_SHARES = (8, 8)
+W2_SHARES = (6, 4)
+W3_SHARES = (0, 0)
+EVEN_SHARE = 3
+LAST_PIECES = ((0, 64, 5), (64, 32, EVEN_SHARE), (96, 32, EVEN_SHARE))
+
+FLOPS = 4 * 2 * PASSES * K_PASS * M * S
 
 
 def tile_picked_zmtp_sigmoid_po_kernel(
@@ -38,165 +46,145 @@ def tile_picked_zmtp_sigmoid_po_kernel(
         psum = ctx.enter_context(tc.psum_pool(name="psum", bufs=1))
 
         def load_list(src, name):
-            lst = keep.tile([P, S // 16], U16, name=name)
-            nc.sync.dma_start(lst[:], src)
-            return lst
-
-        def load_scale_table(src, name):
-            table = keep.tile([P, TABLE], U8, name=name, align_bytes=64)
-            nc.vector.memset(table[:].bitcast(I32), 0)
-            for quad in range(QUADS):
-                nc.sync.dma_start(
-                    out=table[32 * quad : 32 * quad + 4 * PASSES, :].bitcast(I32),
-                    in_=src[:, 4 * quad : 4 * quad + 4, :].bitcast(I32),
-                )
-            return table
+            entries = keep.tile([P, S // 16], U16, name=name)
+            nc.sync.dma_start(entries[:], src)
+            return entries
 
         def load_word_table(src, name):
             table = keep.tile([P, PASSES, TABLE], U32, name=name, align_bytes=64)
             nc.sync.dma_start(
                 out=table[:].bitcast(I32),
-                in_=src.rearrange("g p c r -> p g (c r)").bitcast(I32),
+                in_=src.rearrange("g p c j -> p g (c j)").bitcast(I32),
             )
             return table
 
-        def gather_words(table, lst, name):
-            picked = []
-            for g in range(PASSES):
-                words = keep.tile([P, S], U32, name="%s%d" % (name, g), align_bytes=64)
-                nc.vector.tensor_copy(words[:], table[:, g, :].indirect(lst[:]))
-                picked.append(words)
-            return picked
-
-        def gather_scales(table, lst, name):
-            picked = keep.tile([P, S], U8, name=name, align_bytes=64)
-            nc.vector.tensor_copy(picked[:], table[:].indirect(lst[:]))
-            return picked
-
-        def load_weight(w, g, c0, c1, name):
-            raw = keep.tile([P, PACK, c1 - c0], F32, name=name)
-            rows = w[g * K_PASS : (g + 1) * K_PASS, :].rearrange("(p j) c -> p j c", j=PACK)
-            nc.sync.dma_start(out=raw[:], in_=rows[:, :, c0:c1])
-            return raw
-
-        def weight_tiles(name):
-            grouped = keep.tile([P, PACK, P, PACK], BF16, name=name + "_bf", align_bytes=64)
-            codes = keep.tile([P, M], U32, name=name + "_codes", align_bytes=64)
-            scales = keep.tile([P, M], U8, name=name + "_scales", align_bytes=64)
-            return grouped, codes, scales
-
-        def round_weight(raw, grouped, l0, count, scalar_share):
-            src = raw[:].rearrange("p j (l t) -> p l t j", t=PACK)
-            dst = grouped[:].rearrange("p t l j -> p l t j")
-            nc.scalar.copy(out=dst[:, l0 : l0 + scalar_share], in_=src[:, 0:scalar_share])
-            nc.vector.tensor_copy(out=dst[:, l0 + scalar_share : l0 + count], in_=src[:, scalar_share:count])
-
-        def quantize_whole(tiles):
-            grouped, codes, scales = tiles
-            nc.vector.quantize_mx(
-                out=codes[:].bitcast(FP8X4), scales=scales[:], in_=grouped[:].rearrange("p t l j -> p (t l j)")
-            )
-
-        def quantize_half(tiles, l0):
-            grouped, codes, scales = tiles
-            for t in range(PACK):
-                cols = slice(t * P + l0, t * P + l0 + HALF)
-                nc.vector.quantize_mx(
-                    out=codes[:, cols].bitcast(FP8X4),
-                    scales=scales[:, cols],
-                    in_=grouped[:, t, l0 : l0 + HALF, :].rearrange("p l j -> p (l j)"),
+        def load_scale_table(src, first_row, name):
+            table = keep.tile([P, TABLE], U8, name=name, align_bytes=64)
+            nc.vector.memset(table[:].bitcast(I32), 0)
+            for quad in range(QUADRANTS):
+                row = 32 * quad + first_row
+                nc.gpsimd.dma_start(
+                    out=table[row : row + PASSES * PLANE_ROWS, :].bitcast(I32),
+                    in_=src[:, PLANE_ROWS * quad : PLANE_ROWS * (quad + 1), :].bitcast(I32),
                 )
+            return table
 
-        def whole_weight(w, g, name):
-            raw = load_weight(w, g, 0, M, name + "_raw")
-            tiles = weight_tiles(name)
-            round_weight(raw, tiles[0], 0, P, SCALAR_SHARE)
-            quantize_whole(tiles)
-            return tiles
+        def pick_columns(word_table, scale_table, first_row, entries, name):
+            words = []
+            for g in range(PASSES):
+                picked = keep.tile([P, S], U32, name="%s_words%d" % (name, g), align_bytes=64)
+                nc.vector.tensor_copy(picked[:], word_table[:, g, :].indirect(entries[:]))
+                words.append(picked)
+            planes = keep.tile([P, S], U8, name=name + "_planes", align_bytes=64)
+            nc.vector.tensor_copy(planes[:], scale_table[:].indirect(entries[:]))
+            return [(words[g], planes[first_row + PLANE_ROWS * g : P, :]) for g in range(PASSES)]
 
-        def product(out, tiles, t, words, scales, g, cols, start, stop):
+        def quantised_block(w, g, pieces, name):
+            rows = w[g * K_PASS : (g + 1) * K_PASS, :].rearrange("(p j) m -> p j m", j=PACK)
+            rounded = keep.tile([P, PACK, P, PACK], BF16, name=name + "_rounded", align_bytes=64)
+            codes = keep.tile([P, M], U32, name=name + "_codes", align_bytes=64)
+            plane = keep.tile([P, M], U8, name=name + "_plane", align_bytes=64)
+            for first, places, share in pieces:
+                raw = keep.tile([P, PACK, PACK * places], F32, name="%s_raw%d" % (name, first))
+                nc.sync.dma_start(out=raw[:], in_=rows[:, :, PACK * first : PACK * (first + places)])
+                src = raw[:].rearrange("p j (l t) -> p l j t", t=PACK)
+                dst = rounded[:].rearrange("p t l j -> p l j t")[:, first : first + places]
+                cut = places * share // EIGHTHS
+                if cut > 0:
+                    nc.scalar.copy(out=dst[:, 0:cut], in_=src[:, 0:cut])
+                if cut < places:
+                    nc.vector.tensor_copy(out=dst[:, cut:places], in_=src[:, cut:places])
+            nc.vector.quantize_mx(
+                out=codes[:].bitcast(FP8X4), scales=plane[:], in_=rounded[:].rearrange("p t l j -> p (t l j)")
+            )
+            return codes, plane
+
+        def whole_block(w, g, share, name):
+            return quantised_block(w, g, ((0, P, share),), "%s_%d" % (name, g))
+
+        def product(out, block, t, moving, cols, start, stop):
+            codes, plane = block
+            words, moving_plane = moving
             nc.tensor.matmul_mx(
                 out=out,
-                lhsT=tiles[1][:, t * P : (t + 1) * P].bitcast(FP8X4),
-                lhsT_scale=tiles[2][:, t * P : (t + 1) * P],
-                rhs=words[g][:, cols].bitcast(FP8X4),
-                rhs_scale=scales[4 * g : P, cols],
+                lhsT=codes[:, t * P : (t + 1) * P].bitcast(FP8X4),
+                lhsT_scale=plane[:, t * P : (t + 1) * P],
+                rhs=words[:, cols].bitcast(FP8X4),
+                rhs_scale=moving_plane[:, cols],
                 start=start,
                 stop=stop,
             )
 
         gate_banks = [psum.tile([P, S], F32, name="gate_bank%d" % t) for t in range(PACK)]
-        value_banks = [psum.tile([P, PACK, JQ], F32, name="value_bank%d" % q) for q in range(NQ)]
+        value_banks = [psum.tile([P, PACK, PART], F32, name="value_bank%d" % part) for part in range(PARTS)]
 
-        def gate_pass(tiles, words, scales, g, first, last):
+        def gate_pass(block, moving, first, last):
             for t in range(PACK):
-                product(gate_banks[t][:], tiles, t, words, scales, g, slice(0, S), first, last)
+                product(gate_banks[t][:], block, t, moving, slice(0, S), first, last)
 
-        def value_pass(tiles, words, scales, g, first, last):
-            for q in range(NQ):
+        def value_pass(block, moving, first, last):
+            for part in range(PARTS):
+                cols = slice(part * PART, (part + 1) * PART)
                 for t in range(PACK):
                     product(
-                        value_banks[q][:, t, :], tiles, t, words, scales, g, slice(q * JQ, (q + 1) * JQ),
-                        first and t == 0, last and t == PACK - 1,
+                        value_banks[part][:, t, :], block, t, moving, cols, first and t == 0, last and t == PACK - 1
                     )
 
-        w1_0 = whole_weight(w1, 0, "w1_0")
+        w1_first = whole_block(w1, 0, W1_SHARES[0], "w1")
+        x_word_table = load_word_table(x_words, "x_word_table")
         x_list = load_list(offs, "x_list")
+        e_word_table = load_word_table(e_words, "e_word_table")
         e_list = load_list(tok, "e_list")
-        x_table = load_word_table(x_words, "x_table")
-        x_scale_table = load_scale_table(x_scales, "x_scale_table")
-        x_picked = gather_words(x_table, x_list, "x_picked")
-        x_picked_scales = gather_scales(x_scale_table, x_list, "x_picked_scales")
-        gate_pass(w1_0, x_picked, x_picked_scales, 0, True, False)
-        w1_1 = whole_weight(w1, 1, "w1_1")
-        gate_pass(w1_1, x_picked, x_picked_scales, 1, False, False)
-        e_table = load_word_table(e_words, "e_table")
-        e_scale_table = load_scale_table(e_scales, "e_scale_table")
-        e_picked = gather_words(e_table, e_list, "e_picked")
-        e_picked_scales = gather_scales(e_scale_table, e_list, "e_picked_scales")
-        for g in range(PASSES):
-            w2_g = whole_weight(w2, g, "w2_%d" % g)
-            gate_pass(w2_g, e_picked, e_picked_scales, g, False, g == PASSES - 1)
+        x_scale_table = load_scale_table(x_scales, X_FIRST_ROW, "x_scale_table")
+        e_scale_table = load_scale_table(e_scales, E_FIRST_ROW, "e_scale_table")
+        x = pick_columns(x_word_table, x_scale_table, X_FIRST_ROW, x_list, "x")
+        e = pick_columns(e_word_table, e_scale_table, E_FIRST_ROW, e_list, "e")
 
+        gate_pass(w1_first, x[0], True, False)
+        gate_pass(whole_block(w1, 1, W1_SHARES[1], "w1"), x[1], False, False)
+        for g in range(PASSES):
+            gate_pass(whole_block(w2, g, W2_SHARES[g], "w2"), e[g], False, g == PASSES - 1)
         gate = keep.tile([P, PACK, S], F32, name="gate")
         for t in range(PACK):
             nc.scalar.activation(out=gate[:, t, :], in_=gate_banks[t][:], func=SIGMOID)
 
         for g in range(PASSES):
-            w3_g = whole_weight(w3, g, "w3_%d" % g)
-            value_pass(w3_g, x_picked, x_picked_scales, g, g == 0, False)
-        w4_0 = whole_weight(w4, 0, "w4_0")
-        value_pass(w4_0, e_picked, e_picked_scales, 0, False, False)
-        w4_1 = weight_tiles("w4_1")
-        for h in range(2):
-            raw = load_weight(w4, 1, h * M // 2, (h + 1) * M // 2, "w4_1_raw%d" % h)
-            round_weight(raw, w4_1[0], h * HALF, HALF, SCALAR_SHARE_LAST)
-            quantize_half(w4_1, h * HALF)
-        value_pass(w4_1, e_picked, e_picked_scales, 1, False, True)
+            value_pass(whole_block(w3, g, W3_SHARES[g], "w3"), x[g], g == 0, False)
+        value_pass(whole_block(w4, 0, EVEN_SHARE, "w4"), e[0], False, False)
+        value_pass(quantised_block(w4, 1, LAST_PIECES, "w4_1"), e[1], False, True)
 
-        out_rows = out_0.rearrange("(p t) j -> p t j", t=PACK)
-        out_words = out_1[0].rearrange("p c r -> p (c r)").bitcast(I32)
+        out_rows = out_0.rearrange("(p t) c -> p t c", t=PACK)
+        out_words = out_1[0].rearrange("p c t -> p (c t)").bitcast(I32)
         y_codes = keep.tile([P, S], U32, name="y_codes", align_bytes=64)
-        y_scales = keep.tile([P, S], U8, name="y_scales", align_bytes=64)
-        for q in range(NQ):
-            cols = slice(q * JQ, (q + 1) * JQ)
-            y = keep.tile([P, PACK, JQ], F32, name="y%d" % q)
-            nc.vector.tensor_tensor(out=y[:], in0=value_banks[q][:], in1=gate[:, :, cols], op=MULT)
+        y_plane = keep.tile([P, S], U8, name="y_plane", align_bytes=64)
+        for part in range(PARTS):
+            y = keep.tile([P, PACK, PART], F32, name="y%d" % part)
+            y_rounded = keep.tile([P, PART, PACK], BF16, name="y_rounded%d" % part, align_bytes=64)
+            width = PART // 2 if part == PARTS - 1 else PART
+            for c0 in range(0, PART, width):
+                here = slice(c0, c0 + width)
+                nc.vector.tensor_tensor(
+                    out=y[:, :, here],
+                    in0=value_banks[part][:, :, here],
+                    in1=gate[:, :, part * PART + c0 : part * PART + c0 + width],
+                    op=MULT,
+                )
+                nc.scalar.copy(
+                    out=y_rounded[:, here, :].rearrange("p (c i) t -> p c t i", i=RUN),
+                    in_=y[:, :, here].rearrange("p t (c i) -> p c t i", i=RUN),
+                )
+            cols = slice(part * PART, (part + 1) * PART)
             nc.sync.dma_start(out=out_rows[:, :, cols], in_=y[:])
-            y_bf = keep.tile([P, JQ, PACK], BF16, name="y_bf%d" % q, align_bytes=64)
-            nc.scalar.copy(
-                out=y_bf[:].rearrange("p (c i) t -> p c t i", i=4),
-                in_=y[:].rearrange("p t (c i) -> p c t i", i=4),
-            )
             nc.vector.quantize_mx(
-                out=y_codes[:, cols].bitcast(FP8X4), scales=y_scales[:, cols],
-                in_=y_bf[:].rearrange("p c t -> p (c t)"),
+                out=y_codes[:, cols].bitcast(FP8X4),
+                scales=y_plane[:, cols],
+                in_=y_rounded[:].rearrange("p c t -> p (c t)"),
             )
-        for c0, c1 in ((0, S - JQ), (S - JQ, S)):
-            nc.sync.dma_start(out=out_words[:, c0:c1], in_=y_codes[:, c0:c1].bitcast(I32))
-        for quad in range(QUADS):
+        for cols in (slice(0, S - PART), slice(S - PART, S)):
+            nc.sync.dma_start(out=out_words[:, cols], in_=y_codes[:, cols].bitcast(I32))
+        for quad in range(QUADRANTS):
             queue = nc.sync if quad % 2 == 0 else nc.scalar
             queue.dma_start(
-                out=out_2[0, 4 * quad : 4 * quad + 4, :].bitcast(I32),
-                in_=y_scales[32 * quad : 32 * quad + 4, :].bitcast(I32),
+                out=out_2[0, PLANE_ROWS * quad : PLANE_ROWS * (quad + 1), :].bitcast(I32),
+                in_=y_plane[32 * quad : 32 * quad + PLANE_ROWS, :].bitcast(I32),
             )

from contextlib import ExitStack

import concourse.mybir as mybir

F32 = mybir.dt.float32
BF16 = mybir.dt.bfloat16
I32 = mybir.dt.int32
U32 = mybir.dt.uint32
U16 = mybir.dt.uint16
U8 = mybir.dt.uint8
FP8X4 = mybir.dt.float8_e4m3fn_x4
SIGMOID = mybir.ActivationFunctionType.Sigmoid
MULT = mybir.AluOpType.mult

P = 128
PACK = 4
K_PASS = P * PACK
PASSES = 2
TABLE = 1024
S = 512
M = 512
QUADRANTS = 4
PLANE_ROWS = 4
X_FIRST_ROW = 0
E_FIRST_ROW = 8
PART = 128
PARTS = S // PART
RUN = 4

EIGHTHS = 8
W1_SHARES = (8, 8)
W2_SHARES = (6, 4)
W3_SHARES = (0, 0)
EVEN_SHARE = 3
LAST_PIECES = ((0, 64, 5), (64, 32, EVEN_SHARE), (96, 32, EVEN_SHARE))

FLOPS = 4 * 2 * PASSES * K_PASS * M * S


def tile_picked_zmtp_sigmoid_po_kernel(
    tc, x_words, x_scales, e_words, e_scales, w1, w2, w3, w4, offs, tok, out_0, out_1, out_2
):
    nc = tc.nc
    with ExitStack() as ctx:
        keep = ctx.enter_context(tc.tile_pool(name="keep", bufs=1))
        psum = ctx.enter_context(tc.psum_pool(name="psum", bufs=1))

        def load_list(src, name):
            entries = keep.tile([P, S // 16], U16, name=name)
            nc.sync.dma_start(entries[:], src)
            return entries

        def load_word_table(src, name):
            table = keep.tile([P, PASSES, TABLE], U32, name=name, align_bytes=64)
            nc.sync.dma_start(
                out=table[:].bitcast(I32),
                in_=src.rearrange("g p c j -> p g (c j)").bitcast(I32),
            )
            return table

        def load_scale_table(src, first_row, name):
            table = keep.tile([P, TABLE], U8, name=name, align_bytes=64)
            nc.vector.memset(table[:].bitcast(I32), 0)
            for quad in range(QUADRANTS):
                row = 32 * quad + first_row
                nc.gpsimd.dma_start(
                    out=table[row : row + PASSES * PLANE_ROWS, :].bitcast(I32),
                    in_=src[:, PLANE_ROWS * quad : PLANE_ROWS * (quad + 1), :].bitcast(I32),
                )
            return table

        def pick_columns(word_table, scale_table, first_row, entries, name):
            words = []
            for g in range(PASSES):
                picked = keep.tile([P, S], U32, name="%s_words%d" % (name, g), align_bytes=64)
                nc.vector.tensor_copy(picked[:], word_table[:, g, :].indirect(entries[:]))
                words.append(picked)
            planes = keep.tile([P, S], U8, name=name + "_planes", align_bytes=64)
            nc.vector.tensor_copy(planes[:], scale_table[:].indirect(entries[:]))
            return [(words[g], planes[first_row + PLANE_ROWS * g : P, :]) for g in range(PASSES)]

        def quantised_block(w, g, pieces, name):
            rows = w[g * K_PASS : (g + 1) * K_PASS, :].rearrange("(p j) m -> p j m", j=PACK)
            rounded = keep.tile([P, PACK, P, PACK], BF16, name=name + "_rounded", align_bytes=64)
            codes = keep.tile([P, M], U32, name=name + "_codes", align_bytes=64)
            plane = keep.tile([P, M], U8, name=name + "_plane", align_bytes=64)
            for first, places, share in pieces:
                raw = keep.tile([P, PACK, PACK * places], F32, name="%s_raw%d" % (name, first))
                nc.sync.dma_start(out=raw[:], in_=rows[:, :, PACK * first : PACK * (first + places)])
                src = raw[:].rearrange("p j (l t) -> p l j t", t=PACK)
                dst = rounded[:].rearrange("p t l j -> p l j t")[:, first : first + places]
                cut = places * share // EIGHTHS
                if cut > 0:
                    nc.scalar.copy(out=dst[:, 0:cut], in_=src[:, 0:cut])
                if cut < places:
                    nc.vector.tensor_copy(out=dst[:, cut:places], in_=src[:, cut:places])
            nc.vector.quantize_mx(
                out=codes[:].bitcast(FP8X4), scales=plane[:], in_=rounded[:].rearrange("p t l j -> p (t l j)")
            )
            return codes, plane

        def whole_block(w, g, share, name):
            return quantised_block(w, g, ((0, P, share),), "%s_%d" % (name, g))

        def product(out, block, t, moving, cols, start, stop):
            codes, plane = block
            words, moving_plane = moving
            nc.tensor.matmul_mx(
                out=out,
                lhsT=codes[:, t * P : (t + 1) * P].bitcast(FP8X4),
                lhsT_scale=plane[:, t * P : (t + 1) * P],
                rhs=words[:, cols].bitcast(FP8X4),
                rhs_scale=moving_plane[:, cols],
                start=start,
                stop=stop,
            )

        gate_banks = [psum.tile([P, S], F32, name="gate_bank%d" % t) for t in range(PACK)]
        value_banks = [psum.tile([P, PACK, PART], F32, name="value_bank%d" % part) for part in range(PARTS)]

        def gate_pass(block, moving, first, last):
            for t in range(PACK):
                product(gate_banks[t][:], block, t, moving, slice(0, S), first, last)

        def value_pass(block, moving, first, last):
            for part in range(PARTS):
                cols = slice(part * PART, (part + 1) * PART)
                for t in range(PACK):
                    product(
                        value_banks[part][:, t, :], block, t, moving, cols, first and t == 0, last and t == PACK - 1
                    )

        w1_first = whole_block(w1, 0, W1_SHARES[0], "w1")
        x_word_table = load_word_table(x_words, "x_word_table")
        x_list = load_list(offs, "x_list")
        e_word_table = load_word_table(e_words, "e_word_table")
        e_list = load_list(tok, "e_list")
        x_scale_table = load_scale_table(x_scales, X_FIRST_ROW, "x_scale_table")
        e_scale_table = load_scale_table(e_scales, E_FIRST_ROW, "e_scale_table")
        x = pick_columns(x_word_table, x_scale_table, X_FIRST_ROW, x_list, "x")
        e = pick_columns(e_word_table, e_scale_table, E_FIRST_ROW, e_list, "e")

        gate_pass(w1_first, x[0], True, False)
        gate_pass(whole_block(w1, 1, W1_SHARES[1], "w1"), x[1], False, False)
        for g in range(PASSES):
            gate_pass(whole_block(w2, g, W2_SHARES[g], "w2"), e[g], False, g == PASSES - 1)
        gate = keep.tile([P, PACK, S], F32, name="gate")
        for t in range(PACK):
            nc.scalar.activation(out=gate[:, t, :], in_=gate_banks[t][:], func=SIGMOID)

        for g in range(PASSES):
            value_pass(whole_block(w3, g, W3_SHARES[g], "w3"), x[g], g == 0, False)
        value_pass(whole_block(w4, 0, EVEN_SHARE, "w4"), e[0], False, False)
        value_pass(quantised_block(w4, 1, LAST_PIECES, "w4_1"), e[1], False, True)

        out_rows = out_0.rearrange("(p t) c -> p t c", t=PACK)
        out_words = out_1[0].rearrange("p c t -> p (c t)").bitcast(I32)
        y_codes = keep.tile([P, S], U32, name="y_codes", align_bytes=64)
        y_plane = keep.tile([P, S], U8, name="y_plane", align_bytes=64)
        for part in range(PARTS):
            y = keep.tile([P, PACK, PART], F32, name="y%d" % part)
            y_rounded = keep.tile([P, PART, PACK], BF16, name="y_rounded%d" % part, align_bytes=64)
            width = PART // 2 if part == PARTS - 1 else PART
            for c0 in range(0, PART, width):
                here = slice(c0, c0 + width)
                nc.vector.tensor_tensor(
                    out=y[:, :, here],
                    in0=value_banks[part][:, :, here],
                    in1=gate[:, :, part * PART + c0 : part * PART + c0 + width],
                    op=MULT,
                )
                nc.scalar.copy(
                    out=y_rounded[:, here, :].rearrange("p (c i) t -> p c t i", i=RUN),
                    in_=y[:, :, here].rearrange("p t (c i) -> p c t i", i=RUN),
                )
            cols = slice(part * PART, (part + 1) * PART)
            nc.sync.dma_start(out=out_rows[:, :, cols], in_=y[:])
            nc.vector.quantize_mx(
                out=y_codes[:, cols].bitcast(FP8X4),
                scales=y_plane[:, cols],
                in_=y_rounded[:].rearrange("p c t -> p (c t)"),
            )
        for cols in (slice(0, S - PART), slice(S - PART, S)):
            nc.sync.dma_start(out=out_words[:, cols], in_=y_codes[:, cols].bitcast(I32))
        for quad in range(QUADRANTS):
            queue = nc.sync if quad % 2 == 0 else nc.scalar
            queue.dma_start(
                out=out_2[0, PLANE_ROWS * quad : PLANE_ROWS * (quad + 1), :].bitcast(I32),
                in_=y_plane[32 * quad : 32 * quad + PLANE_ROWS, :].bitcast(I32),
            )
